import numpy as np, ml_dtypes
CORES = [45,53,77,117,47,55,79,119]
N = 8
W, KW, DIL = 256, 5, 4
H = (KW // 2) * DIL
def setup_inputs(rng):
    return {"x": rng.standard_normal((N, 128, W), dtype=np.float32).astype(ml_dtypes.bfloat16), "w": rng.standard_normal((N, 128, KW * 128), dtype=np.float32).astype(ml_dtypes.bfloat16)}
def setup_inputs_big(rng):
    d = setup_inputs(rng)
    for k in ("x", "w"): d[k] = (d[k].astype(np.float32) * 1024.0).astype(d[k].dtype)
    return d
def setup_inputs_small(rng):
    d = setup_inputs(rng)
    for k in ("x", "w"): d[k] = (d[k].astype(np.float32) * (1 / 1024.0)).astype(d[k].dtype)
    return d
def reference(x, w):
    X, W_ = x.astype(np.float64), w.astype(np.float64)
    g = np.concatenate(list(X), axis=1)
    p = np.pad(g, ((0, 0), (H, H)))
    y = np.zeros((N, 128, W))
    for r in range(N):
        for i in range(KW):
            y[r] += W_[r][:, 128 * i:128 * i + 128].T @ p[:, W * r + i * DIL:W * r + i * DIL + W]
    return {"y": y.astype(ml_dtypes.bfloat16 if x.dtype != np.float64 else np.float64)}

@@ -1,0 +1,182 @@
+from concourse.bass import DstId, RemoteDMATransfer
+
+CH, NPOS, TAPS, STEP = 128, 256, 5, 4
+HALO = (TAPS // 2) * STEP
+PAD = NPOS + 2 * HALO
+
+LAND_DIRECT = "dram"
+LAND_PASSED = "sbuf"
+CAP_HAND = 1
+CAP_DIRECT = 16
+CAP_PASSED = 16
+
+SCRATCH = {
+    "xs": ("sbuf", [CH, PAD], "bfloat16"),
+    "ws": ("sbuf", [CH, TAPS * CH], "bfloat16"),
+    "yb": ("sbuf", [CH, NPOS], "bfloat16"),
+    "eo": ("dram", [2, CH, HALO], "bfloat16"),
+    "rb": ("dram", [2, CH, HALO], "bfloat16"),
+    "ld": ("dram", [2, CH, HALO], "bfloat16"),
+    "pm": ("psum", [CH, 512], "float32"),
+    "p0": ("psum", [CH, 512], "float32"),
+    "p1": ("psum", [CH, 512], "float32"),
+}
+SEMAPHORES = ["edge", "inp", "handed", "land0", "land1", "halo0", "halo1", "mid", "side0", "side1", "copied",
+              "stored", "sent"]
+
+
+def _share(topo, src, targets, cap):
+    m = topo.mask(src, targets[0])
+    for t in targets[1:]:
+        m &= topo.mask(src, t)
+    bits = [b for b in range(m.bit_length()) if (m >> b) & 1]
+    n = 1
+    while 2 * n * len(targets) <= len(bits) and 2 * n <= cap:
+        n *= 2
+    return [sum(1 << b for b in bits[k * n:(k + 1) * n]) for k in range(len(targets))], n
+
+
+def _plan(T, topo):
+    cores = list(T.cores)
+    every = range(topo.CHIPS * topo.CORES_PER_CHIP)
+    msgs = []
+    for r, src in enumerate(cores):
+        for s in (0, 1):
+            q = r + (1 if s else -1)
+            if not 0 <= q < len(cores):
+                continue
+            dst = cores[q]
+            via = None
+            if not topo.may_write(src, dst):
+                cand = [c for c in every if c != src and c != dst and topo.chip(c) == topo.chip(src)
+                        and topo.may_write(c, dst)]
+                cand.sort(key=lambda c: (c not in cores, topo.die(c) != topo.die(src), c))
+                via = cand[0]
+            msgs.append({"src": src, "dst": dst, "s": s, "h": 1 - s, "via": via,
+                         "land": LAND_DIRECT if via is None else LAND_PASSED})
+    for c in every:
+        hand = [m for m in msgs if m["src"] == c and m["via"] is not None]
+        direct = [m for m in msgs if m["src"] == c and m["via"] is None]
+        passed = [m for m in msgs if m["via"] == c]
+        assert len(set(m["src"] for m in passed)) <= 1
+        if hand:
+            masks, n = _share(topo, c, [m["via"] for m in hand], CAP_HAND)
+            for m, k in zip(hand, masks):
+                m["mask1"], m["n1"] = k, n
+        for group, cap in ((direct, CAP_DIRECT), (passed, CAP_PASSED)):
+            if group:
+                masks, n = _share(topo, c, [m["dst"] for m in group], cap)
+                for m, k in zip(group, masks):
+                    m["mask2"], m["n2"] = k, n
+    return msgs
+
+
+def _halo(T, h):
+    return T.xs[:, 0:HALO] if h == 0 else T.xs[:, HALO + NPOS:PAD]
+
+
+def _send(g, topo, items, local):
+    if len(items) == 1:
+        d, out, src, rs, mk = items[0]
+        rid, pid = topo.addr(d)[:2]
+        g.remote_dma(out, src, rs, local, pid, rid, mk)
+    else:
+        tr = []
+        for d, out, src, rs, mk in items:
+            rid, pid = topo.addr(d)[:2]
+            tr.append(RemoteDMATransfer(dst_ids=[DstId(rid=rid, pnc=pid)], dma_engine_mask=mk, remote_sem=rs,
+                                        src=src, dst=out))
+        g.remote_dma_fused(tr, local_sem=local)
+    return sum(bin(it[4]).count("1") for it in items)
+
+
+def _last_hop(T, m, src):
+    if m["land"] == "dram":
+        return (m["dst"], T.ld[m["h"]], src, T.sem["land%d" % m["h"]], m["mask2"])
+    return (m["dst"], _halo(T, m["h"]), src, T.sem["halo%d" % m["h"]], m["mask2"])
+
+
+def rank_program(g, core, T, topo):
+    msgs = _plan(T, topo)
+    rank = T.rank_of(core)
+    sem = T.sem
+    passed = [m for m in msgs if m["via"] == core]
+    if rank is None and not passed:
+        return
+    sent = 0
+    dmaq = (g.sync, g.scalar)
+
+    if rank is not None:
+        outs = [m for m in msgs if m["src"] == core]
+        for m in outs:
+            s = m["s"]
+            cols = T.x[:, 0:HALO] if s == 0 else T.x[:, NPOS - HALO:NPOS]
+            dmaq[s].dma_start(T.eo[s], cols).then_inc(sem.edge, 16)
+        g.sync.dma_start(T.xs[:, HALO:HALO + NPOS], T.x[:]).then_inc(sem.inp, 16)
+        g.scalar.dma_start(T.ws[:], T.w[:]).then_inc(sem.inp, 16)
+
+        g.wait_ge(sem.edge, 16 * len(outs))
+        hand = [m for m in outs if m["via"] is not None]
+        direct = [m for m in outs if m["via"] is None]
+        if hand:
+            sent += _send(g, topo, [(m["via"], T.rb[m["s"]], T.eo[m["s"]], sem.handed, m["mask1"]) for m in hand],
+                          sem.sent)
+        if direct:
+            sent += _send(g, topo, [_last_hop(T, m, T.eo[m["s"]]) for m in direct], sem.sent)
+
+    if passed:
+        g.wait_ge(sem.handed, sum(m["n1"] for m in passed))
+        sent += _send(g, topo, [_last_hop(T, m, T.rb[m["s"]]) for m in passed], sem.sent)
+    if sent:
+        g.wait_ge(sem.sent, sent)
+    if rank is None:
+        return
+
+    need, late = [0, 0], [0, 0]
+    for h in (0, 1):
+        got = [m for m in msgs if m["dst"] == core and m["h"] == h]
+        if not got:
+            g.vector.memset(_halo(T, h), 0.0).then_inc(sem["halo%d" % h], 1)
+            need[h], late[h] = 1, (0, 0)
+            continue
+        m = got[0]
+        if m["land"] == "dram":
+            dmaq[h].wait_ge(sem["land%d" % h], m["n2"])
+            dmaq[h].dma_start(_halo(T, h), T.ld[h]).then_inc(sem["halo%d" % h], 16)
+            need[h] = 16
+        else:
+            need[h] = m["n2"]
+        late[h] = (1 if m["via"] is None else 2, -m["n2"])
+    order = sorted((0, 1), key=lambda h: late[h])
+
+    def tap(out, base, width, i, first, last):
+        return g.tensor.matmul(out, T.ws[:, CH * i:CH * (i + 1)], T.xs[:, base + STEP * i:base + STEP * i + width],
+                               first, last)
+
+    bank = (T.p0, T.p1)
+    base = (0, NPOS - HALO)
+    outer = ([i for i in range(TAPS) if STEP * i < HALO],
+             [i for i in range(TAPS) if base[1] + STEP * i + HALO > HALO + NPOS])
+    g.tensor.wait_ge(sem.inp, 32)
+    for i in range(TAPS):
+        mm = tap(T.pm[:, 0:NPOS - 2 * HALO], HALO, NPOS - 2 * HALO, i, i == 0, i == TAPS - 1)
+    mm.then_inc(sem.mid, 1)
+    for h in (0, 1):
+        own = [i for i in range(TAPS) if i not in outer[h]]
+        for i in own:
+            tap(bank[h][:, 0:HALO], base[h], HALO, i, i == own[0], False)
+    for h in order:
+        g.tensor.wait_ge(sem["halo%d" % h], need[h])
+        for i in outer[h]:
+            mm = tap(bank[h][:, 0:HALO], base[h], HALO, i, False, i == outer[h][-1])
+        mm.then_inc(sem["side%d" % h], 1)
+
+    g.vector.wait_ge(sem.mid, 1)
+    g.vector.tensor_copy(T.yb[:, HALO:NPOS - HALO], T.pm[:, 0:NPOS - 2 * HALO]).then_inc(sem.copied, 1)
+    for h in order:
+        g.vector.wait_ge(sem["side%d" % h], 1)
+        g.vector.tensor_copy(T.yb[:, base[h]:base[h] + HALO], bank[h][:, 0:HALO]).then_inc(sem.copied, 1)
+
+    g.sync.wait_ge(sem.copied, 3)
+    g.sync.dma_start(T.y[:], T.yb[:]).then_inc(sem.stored, 16)
+    g.sync.wait_ge(sem.stored, 16)

@@ -1,14 +1,11 @@
-from concourse.bass import DstId, RemoteDMATransfer
-
 CH, NPOS, TAPS, STEP = 128, 256, 5, 4
 HALO = (TAPS // 2) * STEP
 PAD = NPOS + 2 * HALO
 
-LAND_DIRECT = "dram"
-LAND_PASSED = "sbuf"
 CAP_HAND = 1
-CAP_DIRECT = 16
-CAP_PASSED = 16
+CAP_LAST = 16
+CAP_MATE = 8
+LIMIT = 3
 
 SCRATCH = {
     "xs": ("sbuf", [CH, PAD], "bfloat16"),
@@ -16,24 +13,25 @@ SCRATCH = {
     "yb": ("sbuf", [CH, NPOS], "bfloat16"),
     "eo": ("dram", [2, CH, HALO], "bfloat16"),
     "rb": ("dram", [2, CH, HALO], "bfloat16"),
-    "ld": ("dram", [2, CH, HALO], "bfloat16"),
+    "mb": ("dram", [CH, HALO], "bfloat16"),
     "pm": ("psum", [CH, 512], "float32"),
     "p0": ("psum", [CH, 512], "float32"),
     "p1": ("psum", [CH, 512], "float32"),
 }
-SEMAPHORES = ["edge", "inp", "handed", "land0", "land1", "halo0", "halo1", "mid", "side0", "side1", "copied",
-              "stored", "sent"]
+SEMAPHORES = ["edge0", "edge1", "inp", "hand0", "hand1", "mhand", "halo0", "halo1", "mid", "side0", "side1",
+              "cmid", "cside0", "cside1", "clear", "stored", "sent"]
 
 
-def _share(topo, src, targets, cap):
-    m = topo.mask(src, targets[0])
-    for t in targets[1:]:
-        m &= topo.mask(src, t)
-    bits = [b for b in range(m.bit_length()) if (m >> b) & 1]
+def _engines(mask, cap):
+    bits = [b for b in range(mask.bit_length()) if (mask >> b) & 1]
     n = 1
-    while 2 * n * len(targets) <= len(bits) and 2 * n <= cap:
+    while 2 * n <= len(bits) and 2 * n <= cap:
         n *= 2
-    return [sum(1 << b for b in bits[k * n:(k + 1) * n]) for k in range(len(targets))], n
+    return sum(1 << b for b in bits[:n]), n
+
+
+def _ordered(group):
+    return sorted(group, key=lambda m: (m["mate"] is None, -m["urgent"], m["s"]))
 
 
 def _plan(T, topo):
@@ -52,22 +50,33 @@ def _plan(T, topo):
                         and topo.may_write(c, dst)]
                 cand.sort(key=lambda c: (c not in cores, topo.die(c) != topo.die(src), c))
                 via = cand[0]
-            msgs.append({"src": src, "dst": dst, "s": s, "h": 1 - s, "via": via,
-                         "land": LAND_DIRECT if via is None else LAND_PASSED})
+            msgs.append({"src": src, "dst": dst, "s": s, "h": 1 - s, "via": via, "mate": None})
+    for m in msgs:
+        m["urgent"] = len([k for k in msgs if k["dst"] == m["dst"] and k["via"] is not None])
+    for c in cores:
+        own = [m for m in msgs if m["src"] == c and m["via"] is None]
+        over = len(own) + len([m for m in msgs if m["via"] == c]) - LIMIT
+        for m in _ordered(own)[:max(over, 0)]:
+            cand = [k for k in cores if k != c and k != m["dst"] and topo.chip(k) == topo.chip(m["dst"])
+                    and topo.may_write(c, k) and topo.may_write(k, m["dst"])]
+            if cand:
+                m["mate"] = cand[0]
+    for m in msgs:
+        src, dst = m["src"], m["dst"]
+        if m["via"] is not None:
+            m["mask1"], m["n1"] = _engines(topo.mask(src, m["via"]), CAP_HAND)
+            m["mask2"], m["n2"] = _engines(topo.mask(m["via"], dst), CAP_LAST)
+        elif m["mate"] is not None:
+            m["mask1"], m["n1"] = _engines(topo.mask(src, m["mate"]), CAP_HAND)
+            m["mask2"], m["n2"] = _engines(topo.mask(m["mate"], dst), CAP_MATE)
+        else:
+            m["mask2"], m["n2"] = _engines(topo.mask(src, dst), CAP_LAST)
     for c in every:
-        hand = [m for m in msgs if m["src"] == c and m["via"] is not None]
-        direct = [m for m in msgs if m["src"] == c and m["via"] is None]
-        passed = [m for m in msgs if m["via"] == c]
-        assert len(set(m["src"] for m in passed)) <= 1
-        if hand:
-            masks, n = _share(topo, c, [m["via"] for m in hand], CAP_HAND)
-            for m, k in zip(hand, masks):
-                m["mask1"], m["n1"] = k, n
-        for group, cap in ((direct, CAP_DIRECT), (passed, CAP_PASSED)):
-            if group:
-                masks, n = _share(topo, c, [m["dst"] for m in group], cap)
-                for m, k in zip(group, masks):
-                    m["mask2"], m["n2"] = k, n
+        assert len(set(m["src"] for m in msgs if m["via"] == c)) <= 1
+        assert len([m for m in msgs if m["mate"] == c]) <= 1
+    for src in cores:
+        for pos, m in enumerate(_ordered([k for k in msgs if k["src"] == src])):
+            m["pos"] = pos
     return msgs
 
 
@@ -75,58 +84,51 @@ def _halo(T, h):
     return T.xs[:, 0:HALO] if h == 0 else T.xs[:, HALO + NPOS:PAD]
 
 
-def _send(g, topo, items, local):
-    if len(items) == 1:
-        d, out, src, rs, mk = items[0]
-        rid, pid = topo.addr(d)[:2]
-        g.remote_dma(out, src, rs, local, pid, rid, mk)
-    else:
-        tr = []
-        for d, out, src, rs, mk in items:
-            rid, pid = topo.addr(d)[:2]
-            tr.append(RemoteDMATransfer(dst_ids=[DstId(rid=rid, pnc=pid)], dma_engine_mask=mk, remote_sem=rs,
-                                        src=src, dst=out))
-        g.remote_dma_fused(tr, local_sem=local)
-    return sum(bin(it[4]).count("1") for it in items)
-
-
-def _last_hop(T, m, src):
-    if m["land"] == "dram":
-        return (m["dst"], T.ld[m["h"]], src, T.sem["land%d" % m["h"]], m["mask2"])
-    return (m["dst"], _halo(T, m["h"]), src, T.sem["halo%d" % m["h"]], m["mask2"])
-
-
 def rank_program(g, core, T, topo):
     msgs = _plan(T, topo)
     rank = T.rank_of(core)
     sem = T.sem
-    passed = [m for m in msgs if m["via"] == core]
+    passed = _ordered([m for m in msgs if m["via"] == core])
     if rank is None and not passed:
         return
     sent = 0
     dmaq = (g.sync, g.scalar)
 
+    def write(dst, out, src, remote, mask):
+        rid, pid = topo.addr(dst)[:2]
+        g.remote_dma(out, src, remote, sem.sent, pid, rid, mask)
+
     if rank is not None:
-        outs = [m for m in msgs if m["src"] == core]
+        outs = _ordered([m for m in msgs if m["src"] == core])
         for m in outs:
             s = m["s"]
             cols = T.x[:, 0:HALO] if s == 0 else T.x[:, NPOS - HALO:NPOS]
-            dmaq[s].dma_start(T.eo[s], cols).then_inc(sem.edge, 16)
+            dmaq[m["pos"]].dma_start(T.eo[s], cols).then_inc(sem["edge%d" % s], 16)
         g.sync.dma_start(T.xs[:, HALO:HALO + NPOS], T.x[:]).then_inc(sem.inp, 16)
         g.scalar.dma_start(T.ws[:], T.w[:]).then_inc(sem.inp, 16)
 
-        g.wait_ge(sem.edge, 16 * len(outs))
-        hand = [m for m in outs if m["via"] is not None]
-        direct = [m for m in outs if m["via"] is None]
-        if hand:
-            sent += _send(g, topo, [(m["via"], T.rb[m["s"]], T.eo[m["s"]], sem.handed, m["mask1"]) for m in hand],
-                          sem.sent)
-        if direct:
-            sent += _send(g, topo, [_last_hop(T, m, T.eo[m["s"]]) for m in direct], sem.sent)
+        for m in outs:
+            s = m["s"]
+            g.wait_ge(sem["edge%d" % s], 16)
+            if m["via"] is not None:
+                write(m["via"], T.rb[s], T.eo[s], sem["hand%d" % s], m["mask1"])
+                sent += m["n1"]
+            elif m["mate"] is not None:
+                write(m["mate"], T.mb[:], T.eo[s], sem.mhand, m["mask1"])
+                sent += m["n1"]
+            else:
+                write(m["dst"], _halo(T, m["h"]), T.eo[s], sem["halo%d" % m["h"]], m["mask2"])
+                sent += m["n2"]
 
-    if passed:
-        g.wait_ge(sem.handed, sum(m["n1"] for m in passed))
-        sent += _send(g, topo, [_last_hop(T, m, T.rb[m["s"]]) for m in passed], sem.sent)
+    for m in passed:
+        g.wait_ge(sem["hand%d" % m["s"]], m["n1"])
+        write(m["dst"], _halo(T, m["h"]), T.rb[m["s"]], sem["halo%d" % m["h"]], m["mask2"])
+        sent += m["n2"]
+    for m in msgs:
+        if m["mate"] == core:
+            g.wait_ge(sem.mhand, m["n1"])
+            write(m["dst"], _halo(T, m["h"]), T.mb[:], sem["halo%d" % m["h"]], m["mask2"])
+            sent += m["n2"]
     if sent:
         g.wait_ge(sem.sent, sent)
     if rank is None:
@@ -139,15 +141,10 @@ def rank_program(g, core, T, topo):
             g.vector.memset(_halo(T, h), 0.0).then_inc(sem["halo%d" % h], 1)
             need[h], late[h] = 1, (0, 0)
             continue
-        m = got[0]
-        if m["land"] == "dram":
-            dmaq[h].wait_ge(sem["land%d" % h], m["n2"])
-            dmaq[h].dma_start(_halo(T, h), T.ld[h]).then_inc(sem["halo%d" % h], 16)
-            need[h] = 16
-        else:
-            need[h] = m["n2"]
-        late[h] = (1 if m["via"] is None else 2, -m["n2"])
+        need[h] = got[0]["n2"]
+        late[h] = (3 if got[0]["via"] is not None else 2 if got[0]["mate"] is not None else 1, got[0]["pos"])
     order = sorted((0, 1), key=lambda h: late[h])
+    split = max(late)[0] > 1
 
     def tap(out, base, width, i, first, last):
         return g.tensor.matmul(out, T.ws[:, CH * i:CH * (i + 1)], T.xs[:, base + STEP * i:base + STEP * i + width],
@@ -172,11 +169,25 @@ def rank_program(g, core, T, topo):
         mm.then_inc(sem["side%d" % h], 1)
 
     g.vector.wait_ge(sem.mid, 1)
-    g.vector.tensor_copy(T.yb[:, HALO:NPOS - HALO], T.pm[:, 0:NPOS - 2 * HALO]).then_inc(sem.copied, 1)
+    g.vector.tensor_copy(T.yb[:, HALO:NPOS - HALO], T.pm[:, 0:NPOS - 2 * HALO]).then_inc(sem.cmid, 1)
     for h in order:
         g.vector.wait_ge(sem["side%d" % h], 1)
-        g.vector.tensor_copy(T.yb[:, base[h]:base[h] + HALO], bank[h][:, 0:HALO]).then_inc(sem.copied, 1)
+        g.vector.tensor_copy(T.yb[:, base[h]:base[h] + HALO], bank[h][:, 0:HALO]).then_inc(sem["cside%d" % h], 1)
 
-    g.sync.wait_ge(sem.copied, 3)
-    g.sync.dma_start(T.y[:], T.yb[:]).then_inc(sem.stored, 16)
-    g.sync.wait_ge(sem.stored, 16)
+    if not split:
+        g.sync.wait_ge(sem.cmid, 1)
+        for h in order:
+            g.sync.wait_ge(sem["cside%d" % h], 1)
+        g.sync.dma_start(T.y[:], T.yb[:]).then_inc(sem.stored, 16)
+        g.sync.wait_ge(sem.stored, 16)
+        return
+
+    if passed:
+        g.sem_inc(sem.clear, 1)
+        g.sync.wait_ge(sem.clear, 1)
+    g.sync.wait_ge(sem.cmid, 1)
+    g.sync.dma_start(T.y[:, HALO:NPOS - HALO], T.yb[:, HALO:NPOS - HALO]).then_inc(sem.stored, 16)
+    for q, h in zip((g.scalar, g.sync), order):
+        q.wait_ge(sem["cside%d" % h], 1)
+        q.dma_start(T.y[:, base[h]:base[h] + HALO], T.yb[:, base[h]:base[h] + HALO]).then_inc(sem.stored, 16)
+    g.sync.wait_ge(sem.stored, 48)

CH, NPOS, TAPS, STEP = 128, 256, 5, 4
HALO = (TAPS // 2) * STEP
PAD = NPOS + 2 * HALO

CAP_HAND = 1
CAP_LAST = 16
CAP_MATE = 8
LIMIT = 3

SCRATCH = {
    "xs": ("sbuf", [CH, PAD], "bfloat16"),
    "ws": ("sbuf", [CH, TAPS * CH], "bfloat16"),
    "yb": ("sbuf", [CH, NPOS], "bfloat16"),
    "eo": ("dram", [2, CH, HALO], "bfloat16"),
    "rb": ("dram", [2, CH, HALO], "bfloat16"),
    "mb": ("dram", [CH, HALO], "bfloat16"),
    "pm": ("psum", [CH, 512], "float32"),
    "p0": ("psum", [CH, 512], "float32"),
    "p1": ("psum", [CH, 512], "float32"),
}
SEMAPHORES = ["edge0", "edge1", "inp", "hand0", "hand1", "mhand", "halo0", "halo1", "mid", "side0", "side1",
              "cmid", "cside0", "cside1", "clear", "stored", "sent"]


def _engines(mask, cap):
    bits = [b for b in range(mask.bit_length()) if (mask >> b) & 1]
    n = 1
    while 2 * n <= len(bits) and 2 * n <= cap:
        n *= 2
    return sum(1 << b for b in bits[:n]), n


def _ordered(group):
    return sorted(group, key=lambda m: (m["mate"] is None, -m["urgent"], m["s"]))


def _plan(T, topo):
    cores = list(T.cores)
    every = range(topo.CHIPS * topo.CORES_PER_CHIP)
    msgs = []
    for r, src in enumerate(cores):
        for s in (0, 1):
            q = r + (1 if s else -1)
            if not 0 <= q < len(cores):
                continue
            dst = cores[q]
            via = None
            if not topo.may_write(src, dst):
                cand = [c for c in every if c != src and c != dst and topo.chip(c) == topo.chip(src)
                        and topo.may_write(c, dst)]
                cand.sort(key=lambda c: (c not in cores, topo.die(c) != topo.die(src), c))
                via = cand[0]
            msgs.append({"src": src, "dst": dst, "s": s, "h": 1 - s, "via": via, "mate": None})
    for m in msgs:
        m["urgent"] = len([k for k in msgs if k["dst"] == m["dst"] and k["via"] is not None])
    for c in cores:
        own = [m for m in msgs if m["src"] == c and m["via"] is None]
        over = len(own) + len([m for m in msgs if m["via"] == c]) - LIMIT
        for m in _ordered(own)[:max(over, 0)]:
            cand = [k for k in cores if k != c and k != m["dst"] and topo.chip(k) == topo.chip(m["dst"])
                    and topo.may_write(c, k) and topo.may_write(k, m["dst"])]
            if cand:
                m["mate"] = cand[0]
    for m in msgs:
        src, dst = m["src"], m["dst"]
        if m["via"] is not None:
            m["mask1"], m["n1"] = _engines(topo.mask(src, m["via"]), CAP_HAND)
            m["mask2"], m["n2"] = _engines(topo.mask(m["via"], dst), CAP_LAST)
        elif m["mate"] is not None:
            m["mask1"], m["n1"] = _engines(topo.mask(src, m["mate"]), CAP_HAND)
            m["mask2"], m["n2"] = _engines(topo.mask(m["mate"], dst), CAP_MATE)
        else:
            m["mask2"], m["n2"] = _engines(topo.mask(src, dst), CAP_LAST)
    for c in every:
        assert len(set(m["src"] for m in msgs if m["via"] == c)) <= 1
        assert len([m for m in msgs if m["mate"] == c]) <= 1
    for src in cores:
        for pos, m in enumerate(_ordered([k for k in msgs if k["src"] == src])):
            m["pos"] = pos
    return msgs


def _halo(T, h):
    return T.xs[:, 0:HALO] if h == 0 else T.xs[:, HALO + NPOS:PAD]


def rank_program(g, core, T, topo):
    msgs = _plan(T, topo)
    rank = T.rank_of(core)
    sem = T.sem
    passed = _ordered([m for m in msgs if m["via"] == core])
    if rank is None and not passed:
        return
    sent = 0
    dmaq = (g.sync, g.scalar)

    def write(dst, out, src, remote, mask):
        rid, pid = topo.addr(dst)[:2]
        g.remote_dma(out, src, remote, sem.sent, pid, rid, mask)

    if rank is not None:
        outs = _ordered([m for m in msgs if m["src"] == core])
        for m in outs:
            s = m["s"]
            cols = T.x[:, 0:HALO] if s == 0 else T.x[:, NPOS - HALO:NPOS]
            dmaq[m["pos"]].dma_start(T.eo[s], cols).then_inc(sem["edge%d" % s], 16)
        g.sync.dma_start(T.xs[:, HALO:HALO + NPOS], T.x[:]).then_inc(sem.inp, 16)
        g.scalar.dma_start(T.ws[:], T.w[:]).then_inc(sem.inp, 16)

        for m in outs:
            s = m["s"]
            g.wait_ge(sem["edge%d" % s], 16)
            if m["via"] is not None:
                write(m["via"], T.rb[s], T.eo[s], sem["hand%d" % s], m["mask1"])
                sent += m["n1"]
            elif m["mate"] is not None:
                write(m["mate"], T.mb[:], T.eo[s], sem.mhand, m["mask1"])
                sent += m["n1"]
            else:
                write(m["dst"], _halo(T, m["h"]), T.eo[s], sem["halo%d" % m["h"]], m["mask2"])
                sent += m["n2"]

    for m in passed:
        g.wait_ge(sem["hand%d" % m["s"]], m["n1"])
        write(m["dst"], _halo(T, m["h"]), T.rb[m["s"]], sem["halo%d" % m["h"]], m["mask2"])
        sent += m["n2"]
    for m in msgs:
        if m["mate"] == core:
            g.wait_ge(sem.mhand, m["n1"])
            write(m["dst"], _halo(T, m["h"]), T.mb[:], sem["halo%d" % m["h"]], m["mask2"])
            sent += m["n2"]
    if sent:
        g.wait_ge(sem.sent, sent)
    if rank is None:
        return

    need, late = [0, 0], [0, 0]
    for h in (0, 1):
        got = [m for m in msgs if m["dst"] == core and m["h"] == h]
        if not got:
            g.vector.memset(_halo(T, h), 0.0).then_inc(sem["halo%d" % h], 1)
            need[h], late[h] = 1, (0, 0)
            continue
        need[h] = got[0]["n2"]
        late[h] = (3 if got[0]["via"] is not None else 2 if got[0]["mate"] is not None else 1, got[0]["pos"])
    order = sorted((0, 1), key=lambda h: late[h])
    split = max(late)[0] > 1

    def tap(out, base, width, i, first, last):
        return g.tensor.matmul(out, T.ws[:, CH * i:CH * (i + 1)], T.xs[:, base + STEP * i:base + STEP * i + width],
                               first, last)

    bank = (T.p0, T.p1)
    base = (0, NPOS - HALO)
    outer = ([i for i in range(TAPS) if STEP * i < HALO],
             [i for i in range(TAPS) if base[1] + STEP * i + HALO > HALO + NPOS])
    g.tensor.wait_ge(sem.inp, 32)
    for i in range(TAPS):
        mm = tap(T.pm[:, 0:NPOS - 2 * HALO], HALO, NPOS - 2 * HALO, i, i == 0, i == TAPS - 1)
    mm.then_inc(sem.mid, 1)
    for h in (0, 1):
        own = [i for i in range(TAPS) if i not in outer[h]]
        for i in own:
            tap(bank[h][:, 0:HALO], base[h], HALO, i, i == own[0], False)
    for h in order:
        g.tensor.wait_ge(sem["halo%d" % h], need[h])
        for i in outer[h]:
            mm = tap(bank[h][:, 0:HALO], base[h], HALO, i, False, i == outer[h][-1])
        mm.then_inc(sem["side%d" % h], 1)

    g.vector.wait_ge(sem.mid, 1)
    g.vector.tensor_copy(T.yb[:, HALO:NPOS - HALO], T.pm[:, 0:NPOS - 2 * HALO]).then_inc(sem.cmid, 1)
    for h in order:
        g.vector.wait_ge(sem["side%d" % h], 1)
        g.vector.tensor_copy(T.yb[:, base[h]:base[h] + HALO], bank[h][:, 0:HALO]).then_inc(sem["cside%d" % h], 1)

    if not split:
        g.sync.wait_ge(sem.cmid, 1)
        for h in order:
            g.sync.wait_ge(sem["cside%d" % h], 1)
        g.sync.dma_start(T.y[:], T.yb[:]).then_inc(sem.stored, 16)
        g.sync.wait_ge(sem.stored, 16)
        return

    if passed:
        g.sem_inc(sem.clear, 1)
        g.sync.wait_ge(sem.clear, 1)
    g.sync.wait_ge(sem.cmid, 1)
    g.sync.dma_start(T.y[:, HALO:NPOS - HALO], T.yb[:, HALO:NPOS - HALO]).then_inc(sem.stored, 16)
    for q, h in zip((g.scalar, g.sync), order):
        q.wait_ge(sem["cside%d" % h], 1)
        q.dma_start(T.y[:, base[h]:base[h] + HALO], T.yb[:, base[h]:base[h] + HALO]).then_inc(sem.stored, 16)
    g.sync.wait_ge(sem.stored, 48)
